import numpy as np
import ml_dtypes


def mxq(x, axis, fmt="e4m3"):
    dtype, down = {"e4m3": (ml_dtypes.float8_e4m3fn, 7), "e5m2": (ml_dtypes.float8_e5m2, 14)}[fmt]
    v = np.moveaxis(np.asarray(x, np.float32).astype(ml_dtypes.bfloat16).astype(np.float64), axis, -1)
    blocks = v.reshape(v.shape[:-1] + (-1, 32))
    amax = np.abs(blocks).max(-1, keepdims=True)
    byte = np.maximum(np.where(amax > 0, np.frexp(amax)[1] - 1 + 127, 0) - down, 1)
    scale = np.exp2(byte - 127.0)
    codes = (blocks / scale).astype(np.float32).astype(dtype).astype(np.float64)
    return np.moveaxis((codes * scale).reshape(v.shape), -1, axis)


WIDE = False


def mx_kscale(k):
    if not WIDE:
        return np.ones(k)
    levels = np.array([10, -10, 5, -5, 0])
    if k % 512:
        return np.exp2(np.random.permutation(np.resize(levels, k // 32))).repeat(32)
    a = np.empty((k // 512, 16))
    for p in range(k // 512):
        a[p, :8] = np.random.permutation(np.resize(levels, 8))
        for g in range(8):
            far = levels[np.abs(levels - a[p, g]) >= 10]
            a[p, g + 8] = far[np.random.randint(len(far))]
    return np.exp2(a.ravel()).repeat(32)


def f64(x):
    return np.asarray(x).astype(np.float64)


def striped(idx):
    return np.tile(idx.reshape(-1, 16).T, (8, 1)).astype(np.uint16)


def unstriped(offs):
    return offs[:16].T.reshape(-1).astype(np.int64)


E2M1 = np.array([0.0, 0.5, 1.0, 1.5, 2.0, 3.0, 4.0, 6.0, -0.0, -0.5, -1.0, -1.5, -2.0, -3.0, -4.0, -6.0])


def pack_weight(w, fmt):
    k, n = w.shape
    w = f64(np.asarray(w, np.float32).astype(ml_dtypes.bfloat16)).reshape(k // 32, 32, n)
    amax = np.abs(w).max(1)
    if fmt == "e4m3":
        byte = np.frexp(amax)[1] - 1 + 127 - 7
    else:
        mant, ex = np.frexp(amax / 6.0)
        byte = np.where(mant > 0.5, ex, ex - 1) + 127
    byte = np.clip(np.where(amax > 0, byte, 1), 1, 254)
    scaled = (w * np.exp2(127.0 - byte)[:, None, :]).reshape(k, n).astype(np.float32)
    by_word = np.ascontiguousarray(scaled.reshape(k // 512, 128, 4, n).transpose(0, 1, 3, 2))
    if fmt == "e4m3":
        words = by_word.astype(ml_dtypes.float8_e4m3fn).view(np.uint8)
    else:
        c = by_word.astype(ml_dtypes.float4_e2m1fn).view(np.uint8) & 0xF
        words = (c[..., 0::2] | (c[..., 1::2] << 4)).reshape(k // 512, 128, 2 * n)
    return np.ascontiguousarray(words), np.ascontiguousarray(byte.astype(np.uint8).reshape(k // 512, 16, n))


def unpack_weight(words, scales, fmt):
    g, _, n = scales.shape
    words = np.ascontiguousarray(words).reshape(g, 128, n, -1)
    if fmt == "e4m3":
        vals = words.view(ml_dtypes.float8_e4m3fn).astype(np.float64)
    else:
        nib = np.empty((g, 128, n, 4), np.uint8)
        nib[..., 0::2] = words & 0xF
        nib[..., 1::2] = words >> 4
        vals = E2M1[nib]
    vals = vals * np.repeat(np.exp2(scales.astype(np.float64) - 127.0), 8, axis=1)[..., None]
    return vals.transpose(0, 1, 3, 2).reshape(g * 512, n)


def gelu(v):
    return 0.5 * v * (1.0 + np.tanh(np.sqrt(2.0 / np.pi) * (v + 0.044715 * v**3)))


K, K2, T, T3, S, P, H, N = 1024, 512, 4096, 2048, 1024, 512, 512, 768

def setup_inputs():
    n = np.random.standard_normal
    s, s2, u = mx_kscale(K)[:, None], mx_kscale(K2)[:, None], mx_kscale(H)[:, None]
    d = {}
    d["tab_words"], d["tab_scales"] = pack_weight(n((K, T)) * s, "e4m3")
    d["tab2_words"], d["tab2_scales"] = pack_weight(n((K2, T3)) * s2, "e4m3")
    d["offs"] = striped(np.random.permutation(T)[:S])
    d["offs2"] = striped(np.random.permutation(T3)[:P])
    d["pos1"] = striped(np.random.permutation(S)[:P])
    d["w1"] = (n((K, H)) * 0.55 / K**0.5 / s).astype(np.float32)
    d["w2_words"], d["w2_scales"] = pack_weight(n((K2, H)) * 0.56 / K2**0.5 / s2, "e2m1")
    d["wgs"] = np.exp(0.3 * n((128, P))).astype(np.float32)
    d["kz"] = (np.random.uniform(0.6, 1.5, H) * u[:, 0]).astype(np.float32)
    d["base"] = (0.6 * n((H, S)) * u).astype(np.float32)
    d["ks"] = (np.random.uniform(0.6, 1.5, H) * u[:, 0]).astype(np.float32)
    d["wz"] = (n((H, N)) / H**0.5 / u).astype(np.float32)
    d["ws_words"], d["ws_scales"] = pack_weight(n((H, N)) * 2.4 / H**0.5 / u, "e4m3")
    return d

def reference(tab_words, tab_scales, tab2_words, tab2_scales, offs, offs2, pos1, w1,
              w2_words, w2_scales, wgs, kz, base, ks, wz, ws_words, ws_scales):
    v = unpack_weight(tab_words, tab_scales, "e4m3")[:, unstriped(offs)]
    v2 = unpack_weight(tab2_words, tab2_scales, "e4m3")[:, unstriped(offs2)]
    w2 = unpack_weight(w2_words, w2_scales, "e2m1")
    ws = unpack_weight(ws_words, ws_scales, "e4m3")
    a = mxq(f64(w1), 0, "e4m3").T @ v
    b0 = w2.T @ v2
    b = np.maximum(b0, np.cos(b0))
    placed = np.zeros((H, S))
    placed[:, unstriped(pos1)] = np.tile(f64(wgs), (H // 128, 1)) * b
    z = np.maximum(a, placed) * f64(kz)[:, None] + f64(base)
    x = np.sin(a) * f64(ks)[:, None]
    y = mxq(f64(wz), 0, "e4m3").T @ mxq(z, 0, "e4m3") + ws.T @ mxq(x, 0, "e4m3")
    return y / (1.0 + np.exp(-y))

@@ -1,0 +1,324 @@
+import math
+from contextlib import ExitStack
+
+import concourse.mybir as mybir
+
+K, K2, T, T3, S, L, H, N = 1024, 512, 4096, 2048, 1024, 512, 512, 768
+FLOPS = 2 * (K * H * S + K2 * H * L + 2 * H * N * S)
+
+F32 = mybir.dt.float32
+BF16 = mybir.dt.bfloat16
+I32 = mybir.dt.int32
+U32 = mybir.dt.uint32
+U16 = mybir.dt.uint16
+U8 = mybir.dt.uint8
+FP8X4 = mybir.dt.float8_e4m3fn_x4
+FP4X4 = mybir.dt.float4_e2m1fn_x4
+ALU = mybir.AluOpType
+ACT = mybir.ActivationFunctionType
+
+P = 128
+PACK = 4
+HALF = 512
+CHUNK = 256
+TWO_PI = 2.0 * math.pi
+ROUNDER = 1.5 * 2.0**23
+KB_V = 2
+KA_V = 0
+XIL_V = ()
+ZIL_S = ()
+GATES = (0, 3, 5)
+TOPS = ("x_rows0", "b0", "x_rows1", "x_rows1")
+Z1_AFTER = "z_rows0"
+FINE = 1
+ORDER = "atb"
+Y_BANKS = ((4, 5, 6), (7, 4, 5), (0, 1, 2), (3, 6, 7))
+
+
+def tile_list_ballast_survival_scorer_kernel(
+    tc, tab_words, tab_scales, tab2_words, tab2_scales, offs, offs2, pos1, w1,
+    w2_words, w2_scales, wgs, kz, base, ks, wz, ws_words, ws_scales, out,
+):
+    nc = tc.nc
+    with ExitStack() as ctx:
+        keep = ctx.enter_context(tc.tile_pool(name="keep", bufs=1))
+        ring = ctx.enter_context(tc.tile_pool(name="ring", bufs=3))
+        psum = ctx.enter_context(tc.psum_pool(name="psum", bufs=1))
+
+        def held(name, shape, dtype, after=None):
+            return keep.tile(shape, dtype, name=name, tag=after or name, align_bytes=64)
+
+        def bank(index, name, shape):
+            return psum.tile(shape, F32, name=name, tag="bank%d" % index)
+
+        def zero_bytes(tile):
+            nc.vector.memset(tile[:].bitcast(I32), 0)
+
+        def load_scale_rows(queue, plane, scales):
+            passes = scales.shape[0]
+            for q in range(4):
+                if passes == 1:
+                    src = scales[0, 4 * q : 4 * q + 4, :]
+                else:
+                    src = scales[:, 4 * q : 4 * q + 4, :]
+                queue.dma_start(out=plane[32 * q : 32 * q + 4 * passes, :].bitcast(I32), in_=src.bitcast(I32))
+
+        def load_words(tile, words):
+            nc.sync.dma_start(out=tile[:], in_=words.rearrange("p n t -> p (n t)").bitcast(I32))
+
+        offs_t = keep.tile([P, S // 16], U16, name="offs_t")
+        offs2_t = keep.tile([P, L // 16], U16, name="offs2_t")
+        pos_t = keep.tile([P, L // 16], U16, name="pos_t")
+        tab2_plane = held("tab2_plane", [P, T3], U8)
+        w2_plane = held("w2_plane", [P, H], U8)
+        tab_plane = held("tab_plane", [P, T], U8)
+        placed = [held("placed%d" % t, [P, S], F32) for t in range(PACK)]
+        warm = held("warm", [P, 2], F32)
+
+        zero_bytes(tab2_plane)
+        zero_bytes(w2_plane)
+        nc.vector.memset(warm[:, 0:1], 0.0)
+        nc.scalar.activation(out=warm[:, 1:2], in_=warm[:, 0:1], func=ACT.Silu)
+        zero_bytes(tab_plane)
+        for page in placed:
+            nc.gpsimd.memset(page[:], 0.0)
+
+        tab2_w = held("tab2_w", [P, T3], I32)
+        w2_w = held("w2_w", [P, 2 * H], U8)
+        tab_w = [held("tab_w0", [P, T], I32)]
+        w1_raw = [keep.tile([P, PACK, H], F32, name="w1_raw%d" % a, tag="wraw", bufs=2) for a in range(2)]
+        def big(which):
+            if which == "t":
+                load_words(tab_w[0], tab_words[0])
+            else:
+                a = 0 if which == "a" else 1
+                nc.sync.dma_start(out=w1_raw[a][:], in_=w1[512 * a : 512 * a + 512, :].rearrange("(p j) c -> p j c", j=PACK))
+
+        nc.sync.dma_start(out=offs2_t[:], in_=offs2)
+        nc.sync.dma_start(out=w2_w[:].bitcast(I32), in_=w2_words[0].bitcast(I32))
+        load_scale_rows(nc.sync, tab2_plane, tab2_scales)
+        load_words(tab2_w, tab2_words[0])
+        load_scale_rows(nc.sync, w2_plane, w2_scales)
+        big(ORDER[0])
+        nc.sync.dma_start(out=offs_t[:], in_=offs)
+        load_scale_rows(nc.sync, tab_plane, tab_scales)
+        big(ORDER[1])
+        big(ORDER[2])
+        wz_raw = [keep.tile([P, PACK, N // 2], F32, name="wz_raw%d" % u, tag="wraw", bufs=2) for u in range(2)]
+
+        w2_dealt = held("w2_dealt", [P, 2 * H], U8)
+        nc.vector.tensor_copy(
+            out=w2_dealt[:].rearrange("p (t m b) -> p t m b", t=PACK, b=2),
+            in_=w2_w[:].rearrange("p (m t b) -> p t m b", t=PACK, b=2),
+        )
+        tab_w.append(held("tab_w1", [P, T], I32, after="w2_w"))
+        load_words(tab_w[1], tab_words[1])
+        v2_scales = held("v2_scales", [P, L], U8)
+        nc.vector.tensor_copy(out=v2_scales[:], in_=tab2_plane[:].indirect(offs2_t[:]))
+        wgs_t = held("wgs_t", [P, PACK, L], F32, after="tab2_plane")
+        for q in range(4):
+            nc.sync.dma_start(out=wgs_t[32 * q : 32 * q + 32, :, :], in_=wgs.rearrange("(p t) j -> p t j", t=PACK))
+        nc.sync.dma_start(out=pos_t[:], in_=pos1)
+        kz_t = held("kz_t", [P, PACK], F32)
+        ks_t = held("ks_t", [P, PACK], F32)
+        nc.sync.dma_start(out=ks_t[:], in_=ks.rearrange("(p t) -> p t", t=PACK))
+        nc.sync.dma_start(out=kz_t[:], in_=kz.rearrange("(p t) -> p t", t=PACK))
+        v2_words = held("v2_words", [P, L], U32)
+        nc.vector.tensor_copy(out=v2_words[:], in_=tab2_w[:].bitcast(U32).indirect(offs2_t[:]))
+        w2_dealt_plane = held("w2_dealt_plane", [P, H], U8)
+        nc.vector.tensor_copy(
+            out=w2_dealt_plane[:].rearrange("p (t m) -> p t m", t=PACK),
+            in_=w2_plane[:].rearrange("p (m t) -> p t m", t=PACK),
+        )
+
+        def turns_and_whole(acc, shift, slot, on_vector):
+            turns = keep.tile([P, HALF], F32, name="turns", tag="turns%d" % slot)
+            nc.scalar.activation(out=turns[:], in_=acc[:], func=ACT.Copy, scale=1.0 / TWO_PI, bias=shift)
+            whole = keep.tile([P, HALF], I32, name="whole", tag="whole%d" % slot)
+            if on_vector:
+                nc.vector.tensor_scalar(out=whole[:], in0=turns[:], scalar1=ROUNDER, scalar2=None, op0=ALU.add)
+            else:
+                nc.scalar.activation(out=whole[:].bitcast(U32), in_=turns[:], func=ACT.Copy, bias=ROUNDER)
+            return turns, whole
+
+        def sine_of(turns, whole):
+            nc.vector.scalar_tensor_tensor(
+                out=turns[:], in0=whole[:], scalar=ROUNDER, in1=turns[:],
+                op0=ALU.subtract, op1=ALU.subtract,
+            )
+            nc.scalar.activation(out=turns[:], in_=turns[:], func=ACT.Sin, scale=-TWO_PI)
+            return turns
+
+        b = [held("b%d" % t, [P, L], F32) for t in range(PACK)]
+        b0 = []
+        for t in range(PACK):
+            acc = bank(t, "b0_%d" % t, [P, L])
+            nc.tensor.matmul_mx(
+                out=acc[:],
+                lhsT=w2_dealt[:, 2 * P * t : 2 * P * (t + 1)].bitcast(FP4X4),
+                lhsT_scale=w2_dealt_plane[:, P * t : P * (t + 1)],
+                rhs=v2_words[:].bitcast(FP8X4),
+                rhs_scale=v2_scales[:],
+                start=True, stop=True,
+            )
+            b0.append(acc)
+        base_rows = base.rearrange("(p t) j -> p t j", t=PACK)
+        base_t = []
+        for t, freed in enumerate(("tab2_w", "w2_plane", "w2_dealt", "v2_words")):
+            rows = held("base%d" % t, [P, S], F32, after=freed)
+            nc.sync.dma_start(out=rows[:], in_=base_rows[:, t, :])
+            base_t.append(rows)
+        ws_w = held("ws_w", [P, N], I32, after="w2_dealt_plane")
+        load_words(ws_w, ws_words[0])
+        ws_plane = held("ws_plane", [P, N], U8, after="v2_scales")
+        nc.gpsimd.memset(ws_plane[:].bitcast(I32), 0)
+        load_scale_rows(nc.sync, ws_plane, ws_scales)
+        for t in range(PACK):
+            cosine = sine_of(*turns_and_whole(b0[t], 0.25, t, t < KB_V))
+            nc.vector.tensor_tensor(out=b[t][:], in0=b0[t][:], in1=cosine[:], op=ALU.max)
+
+        w1_codes, w1_plane, v_words = [], [], []
+        w1_grouped = held("grouped", [P, 2, H * PACK], BF16)
+        v_scales = held("v_scales", [P, S], U8)
+        for h in range(2):
+            nc.vector.tensor_copy(
+                out=v_scales[:, HALF * h : HALF * (h + 1)], in_=tab_plane[:].indirect(offs_t[:, 32 * h : 32 * h + 32])
+            )
+        for a in range(2):
+            grouped = w1_grouped[:, a, :]
+            for m0 in (0, 64):
+                nc.scalar.copy(
+                    out=grouped.rearrange("p (t m j) -> p m j t", t=PACK, j=PACK)[:, m0 : m0 + 64],
+                    in_=w1_raw[a][:].rearrange("p j (m t) -> p m j t", t=PACK)[:, m0 : m0 + 64],
+                )
+            codes = held("w1_codes%d" % a, [P, H], U32)
+            plane = held("w1_plane%d" % a, [P, H], U8)
+            nc.vector.quantize_mx(out=codes[:].bitcast(FP8X4), scales=plane[:], in_=grouped)
+            w1_codes.append(codes)
+            w1_plane.append(plane)
+            halves = []
+            for h in range(2):
+                words = held("v_words%d_%d" % (a, h), [P, HALF], U32)
+                nc.vector.tensor_copy(
+                    out=words[:], in_=tab_w[a][:].bitcast(U32).indirect(offs_t[:, 32 * h : 32 * h + 32])
+                )
+                halves.append(words)
+            v_words.append(halves)
+
+        a_acc = {}
+        for h in range(2):
+            for t in range(PACK):
+                acc = bank(4 * (1 - h) + t, "a_%d_%d" % (h, t), [P, HALF])
+                for a in range(2):
+                    nc.tensor.matmul_mx(
+                        out=acc[:],
+                        lhsT=w1_codes[a][:, P * t : P * (t + 1)].bitcast(FP8X4),
+                        lhsT_scale=w1_plane[a][:, P * t : P * (t + 1)],
+                        rhs=v_words[a][h][:].bitcast(FP8X4),
+                        rhs_scale=v_scales[4 * a : P, HALF * h : HALF * (h + 1)],
+                        start=(a == 0), stop=(a == 1),
+                    )
+                a_acc[(h, t)] = acc
+
+        def interleave(engine_copy, dst, src):
+            engine_copy(
+                out=dst.rearrange("p (c i t) -> p c t i", i=4, t=PACK),
+                in_=src.rearrange("p t (c i) -> p c t i", i=4),
+            )
+
+        for u in range(2):
+            nc.sync.dma_start(
+                out=wz_raw[u][:], in_=wz[:, 384 * u : 384 * (u + 1)].rearrange("(p j) c -> p j c", j=PACK)
+            )
+        wz_grouped = held("wz_grouped", [P, N * PACK], BF16)
+        wz_codes = held("wz_codes", [P, N], U32)
+        wz_plane = held("wz_plane", [P, N], U8)
+
+        def prepare_wz():
+            for u in range(2):
+                interleave(nc.scalar.copy, wz_grouped[:, 1536 * u : 1536 * (u + 1)], wz_raw[u][:])
+            for lo, hi in ((0, 512), (512, 768)):
+                nc.vector.quantize_mx(
+                    out=wz_codes[:, lo:hi].bitcast(FP8X4), scales=wz_plane[:, lo:hi],
+                    in_=wz_grouped[:, PACK * lo : PACK * hi],
+                )
+
+        x_rows = [held("x_rows%d" % h, [P, PACK, HALF], BF16) for h in range(2)]
+        z_rows = [held("z_rows0", [P, PACK, HALF], BF16)]
+        x_codes = [held("x_codes%d" % h, [P, HALF], U32) for h in range(2)]
+        x_plane = [held("x_plane%d" % h, [P, HALF], U8) for h in range(2)]
+
+        def x_part(h, t):
+            sine = sine_of(*reduced[(h, t)])
+            nc.scalar.activation(out=x_rows[h][:, t, :], in_=sine[:], func=ACT.Copy, scale=ks_t[:, t : t + 1])
+
+        def x_finish(h):
+            grouped = held("x_grouped%d" % h, [P, HALF * PACK], BF16)
+            interleave(nc.vector.tensor_copy if h in XIL_V else nc.scalar.copy, grouped[:], x_rows[h][:])
+            nc.vector.quantize_mx(out=x_codes[h][:].bitcast(FP8X4), scales=x_plane[h][:], in_=grouped[:])
+
+        def scatter(t):
+            nc.vector.tensor_tensor(
+                out=placed[t][:].indirect(pos_t[:]), in0=b[t][:], in1=wgs_t[:, t, :], op=ALU.mult
+            )
+
+        def z_part(t, lo, width, top):
+            h, at = divmod(lo, HALF)
+            nc.vector.tensor_tensor(
+                out=top[:, 0:width], in0=a_acc[(h, t)][:, at : at + width], in1=placed[t][:, lo : lo + width], op=ALU.max
+            )
+            nc.vector.scalar_tensor_tensor(
+                out=z_rows[h][:, t, at : at + width], in0=top[:, 0:width], scalar=kz_t[:, t : t + 1],
+                in1=base_t[t][:, lo : lo + width], op0=ALU.mult, op1=ALU.add,
+            )
+
+        reduced = {}
+        for h in range(2):
+            for t in range(PACK):
+                reduced[(h, t)] = turns_and_whole(a_acc[(h, t)], 0.0, PACK * h + t, PACK * h + t < KA_V)
+        prepare_wz()
+        for h in range(2):
+            for t in range(PACK):
+                x_part(h, t)
+            x_finish(h)
+        for t in range(PACK):
+            scatter(t)
+        results = held("results", [P, 12, 2, CHUNK], F32, after="x_rows1")
+
+        out_rows = out.rearrange("(g p) j -> p g j", p=P)
+        for c in range(S // CHUNK):
+            lo = CHUNK * c
+            h, at = divmod(lo, HALF)
+            if c == 2:
+                z_rows.append(held("z_rows1", [P, PACK, HALF], BF16, after=Z1_AFTER))
+            if c == 0 or (c == 2 and not FINE):
+                for t in range(PACK - 1):
+                    z_part(t, lo, HALF, ring.tile([P, HALF], F32, name="top", bufs=2))
+            if h == 1 and FINE:
+                for t in range(PACK - 1):
+                    z_part(t, lo, CHUNK, ring.tile([P, HALF], F32, name="top", bufs=2))
+            z_part(PACK - 1, lo, CHUNK, ring.tile([P, HALF], F32, name="top", bufs=2))
+            grouped = held("z_grouped", [P, CHUNK * PACK], BF16, after="x_grouped%d" % h)
+            interleave(nc.scalar.copy if c in ZIL_S else nc.vector.tensor_copy, grouped[:], z_rows[h][:, :, at : at + CHUNK])
+            z_codes = ring.tile([P, CHUNK], U32, name="z_codes", bufs=2, align_bytes=64)
+            z_plane = ring.tile([P, CHUNK], U8, name="z_plane", bufs=2, align_bytes=64)
+            nc.vector.quantize_mx(out=z_codes[:].bitcast(FP8X4), scales=z_plane[:], in_=grouped[:])
+            for g in range(3):
+                acc = bank(Y_BANKS[c][g], "y_%d_%d" % (c, g), [P, 2, CHUNK])
+                for u in range(2):
+                    cols = slice(P * (2 * g + u), P * (2 * g + u + 1))
+                    nc.tensor.matmul_mx(
+                        out=acc[:, u, :], lhsT=ws_w[:, cols].bitcast(FP8X4), lhsT_scale=ws_plane[:, cols],
+                        rhs=x_codes[h][:, at : at + CHUNK].bitcast(FP8X4), rhs_scale=x_plane[h][:, at : at + CHUNK],
+                        start=(u == 0), stop=False,
+                    )
+                for u in range(2):
+                    cols = slice(P * (2 * g + u), P * (2 * g + u + 1))
+                    nc.tensor.matmul_mx(
+                        out=acc[:, u, :], lhsT=wz_codes[:, cols].bitcast(FP8X4), lhsT_scale=wz_plane[:, cols],
+                        rhs=z_codes[:].bitcast(FP8X4), rhs_scale=z_plane[:],
+                        start=False, stop=(u == 1),
+                    )
+                result = results[:, 3 * c + g]
+                nc.scalar.activation(out=result, in_=acc[:], func=ACT.Silu)
+                nc.sync.dma_start(out=out_rows[:, 2 * g : 2 * g + 2, lo : lo + CHUNK], in_=result)

@@ -80,13 +80,11 @@ def tile_list_ballast_survival_scorer_kernel(
         nc.vector.memset(warm[:, 0:1], 0.0)
         nc.scalar.activation(out=warm[:, 1:2], in_=warm[:, 0:1], func=ACT.Silu)
         zero_bytes(tab_plane)
-        for page in placed:
-            nc.gpsimd.memset(page[:], 0.0)
 
         tab2_w = held("tab2_w", [P, T3], I32)
         w2_w = held("w2_w", [P, 2 * H], U8)
         tab_w = [held("tab_w0", [P, T], I32)]
-        w1_raw = [keep.tile([P, PACK, H], F32, name="w1_raw%d" % a, tag="wraw", bufs=2) for a in range(2)]
+        w1_raw = [held("w1_raw%d" % a, [P, PACK, H], F32) for a in range(2)]
         def big(which):
             if which == "t":
                 load_words(tab_w[0], tab_words[0])
@@ -104,7 +102,6 @@ def tile_list_ballast_survival_scorer_kernel(
         load_scale_rows(nc.sync, tab_plane, tab_scales)
         big(ORDER[1])
         big(ORDER[2])
-        wz_raw = [keep.tile([P, PACK, N // 2], F32, name="wz_raw%d" % u, tag="wraw", bufs=2) for u in range(2)]
 
         w2_dealt = held("w2_dealt", [P, 2 * H], U8)
         nc.vector.tensor_copy(
@@ -162,16 +159,25 @@ def tile_list_ballast_survival_scorer_kernel(
                 start=True, stop=True,
             )
             b0.append(acc)
+        wz_raw = []
+        for u, freed in enumerate(("tab2_w", "w2_plane")):
+            raw = held("wz_raw%d" % u, [P, PACK, N // 2], F32, after=freed)
+            nc.sync.dma_start(out=raw[:], in_=wz[:, 384 * u : 384 * (u + 1)].rearrange("(p j) c -> p j c", j=PACK))
+            wz_raw.append(raw)
         base_rows = base.rearrange("(p t) j -> p t j", t=PACK)
         base_t = []
-        for t, freed in enumerate(("tab2_w", "w2_plane", "w2_dealt", "v2_words")):
-            rows = held("base%d" % t, [P, S], F32, after=freed)
-            nc.sync.dma_start(out=rows[:], in_=base_rows[:, t, :])
+
+        def load_base(freed):
+            rows = held("base", [P, S], F32, after=freed)
+            nc.sync.dma_start(out=rows[:], in_=base_rows[:, len(base_t), :])
             base_t.append(rows)
+
+        load_base("w2_dealt")
+        load_base("v2_words")
         ws_w = held("ws_w", [P, N], I32, after="w2_dealt_plane")
         load_words(ws_w, ws_words[0])
         ws_plane = held("ws_plane", [P, N], U8, after="v2_scales")
-        nc.gpsimd.memset(ws_plane[:].bitcast(I32), 0)
+        zero_bytes(ws_plane)
         load_scale_rows(nc.sync, ws_plane, ws_scales)
         for t in range(PACK):
             cosine = sine_of(*turns_and_whole(b0[t], 0.25, t, t < KB_V))
@@ -188,8 +194,8 @@ def tile_list_ballast_survival_scorer_kernel(
             grouped = w1_grouped[:, a, :]
             for m0 in (0, 64):
                 nc.scalar.copy(
-                    out=grouped.rearrange("p (t m j) -> p m j t", t=PACK, j=PACK)[:, m0 : m0 + 64],
-                    in_=w1_raw[a][:].rearrange("p j (m t) -> p m j t", t=PACK)[:, m0 : m0 + 64],
+                    out=grouped.rearrange("p (t m j) -> p m t j", t=PACK, j=PACK)[:, m0 : m0 + 64],
+                    in_=w1_raw[a][:].rearrange("p j (m t) -> p m t j", t=PACK)[:, m0 : m0 + 64],
                 )
             codes = held("w1_codes%d" % a, [P, H], U32)
             plane = held("w1_plane%d" % a, [P, H], U8)
@@ -226,10 +232,8 @@ def tile_list_ballast_survival_scorer_kernel(
                 in_=src.rearrange("p t (c i) -> p c t i", i=4),
             )
 
-        for u in range(2):
-            nc.sync.dma_start(
-                out=wz_raw[u][:], in_=wz[:, 384 * u : 384 * (u + 1)].rearrange("(p j) c -> p j c", j=PACK)
-            )
+        load_base("w1_raw0")
+        load_base("w1_raw1")
         wz_grouped = held("wz_grouped", [P, N * PACK], BF16)
         wz_codes = held("wz_codes", [P, N], U32)
         wz_plane = held("wz_plane", [P, N], U8)
@@ -282,6 +286,7 @@ def tile_list_ballast_survival_scorer_kernel(
                 x_part(h, t)
             x_finish(h)
         for t in range(PACK):
+            nc.vector.memset(placed[t][:], 0.0)
             scatter(t)
         results = held("results", [P, 12, 2, CHUNK], F32, after="x_rows1")
 

@@ -29,8 +29,14 @@ XIL_V = ()
 ZIL_S = ()
 GATES = (0, 3, 5)
 TOPS = ("x_rows0", "b0", "x_rows1", "x_rows1")
-Z1_AFTER = "z_rows0"
+Z1_AFTER = "x_rows0"
 FINE = 1
+LATE = 2
+PIECES = (((0, 256, (4, 5, 6)),), ((256, 256, (7, 4, 5)),), ((512, 256, (6, 7, 4)),), ((768, 256, (0, 1, 2)),))
+GATE = "x_rows1"
+TWOQ = 1
+HEAD = "ows2WaOStb"
+EARLY = 1
 ORDER = "atb"
 Y_BANKS = ((4, 5, 6), (7, 4, 5), (0, 1, 2), (3, 6, 7))
 
@@ -54,9 +60,10 @@ def tile_list_ballast_survival_scorer_kernel(
         def zero_bytes(tile):
             nc.vector.memset(tile[:].bitcast(I32), 0)
 
-        def load_scale_rows(queue, plane, scales):
+        def load_scale_rows(queues, plane, scales):
             passes = scales.shape[0]
-            for q in range(4):
+            for q in (0, 2, 1, 3):
+                queue = queues[q // 2]
                 if passes == 1:
                     src = scales[0, 4 * q : 4 * q + 4, :]
                 else:
@@ -72,14 +79,13 @@ def tile_list_ballast_survival_scorer_kernel(
         tab2_plane = held("tab2_plane", [P, T3], U8)
         w2_plane = held("w2_plane", [P, H], U8)
         tab_plane = held("tab_plane", [P, T], U8)
-        placed = [held("placed%d" % t, [P, S], F32) for t in range(PACK)]
+        placed = [held("placed%d" % t, [P, S], F32) for t in range(PACK - LATE)]
         warm = held("warm", [P, 2], F32)
 
         zero_bytes(tab2_plane)
         zero_bytes(w2_plane)
-        nc.vector.memset(warm[:, 0:1], 0.0)
-        nc.scalar.activation(out=warm[:, 1:2], in_=warm[:, 0:1], func=ACT.Silu)
         zero_bytes(tab_plane)
+        ws_plane = held("ws_plane", [P, N], U8)
 
         tab2_w = held("tab2_w", [P, T3], I32)
         w2_w = held("w2_w", [P, 2 * H], U8)
@@ -92,30 +98,47 @@ def tile_list_ballast_survival_scorer_kernel(
                 a = 0 if which == "a" else 1
                 nc.sync.dma_start(out=w1_raw[a][:], in_=w1[512 * a : 512 * a + 512, :].rearrange("(p j) c -> p j c", j=PACK))
 
-        nc.sync.dma_start(out=offs2_t[:], in_=offs2)
-        nc.sync.dma_start(out=w2_w[:].bitcast(I32), in_=w2_words[0].bitcast(I32))
-        load_scale_rows(nc.sync, tab2_plane, tab2_scales)
-        load_words(tab2_w, tab2_words[0])
-        load_scale_rows(nc.sync, w2_plane, w2_scales)
-        big(ORDER[0])
-        nc.sync.dma_start(out=offs_t[:], in_=offs)
-        load_scale_rows(nc.sync, tab_plane, tab_scales)
-        big(ORDER[1])
-        big(ORDER[2])
+        second = nc.scalar if TWOQ else nc.sync
+        for which in HEAD:
+            if which == "o":
+                nc.sync.dma_start(out=offs2_t[:], in_=offs2)
+            elif which == "O":
+                nc.sync.dma_start(out=offs_t[:], in_=offs)
+            elif which == "s":
+                load_scale_rows((nc.sync, second), tab2_plane, tab2_scales)
+            elif which == "S":
+                load_scale_rows((nc.sync, second), tab_plane, tab_scales)
+            elif which == "2":
+                load_words(tab2_w, tab2_words[0])
+            elif which == "w":
+                nc.sync.dma_start(out=w2_w[:].bitcast(I32), in_=w2_words[0].bitcast(I32))
+            elif which == "W":
+                load_scale_rows((nc.sync, nc.sync), w2_plane, w2_scales)
+            else:
+                big(which)
+        nc.vector.memset(warm[:, 0:1], 0.0)
+        nc.scalar.activation(out=warm[:, 1:2], in_=warm[:, 0:1], func=ACT.Silu)
 
         w2_dealt = held("w2_dealt", [P, 2 * H], U8)
         nc.vector.tensor_copy(
             out=w2_dealt[:].rearrange("p (t m b) -> p t m b", t=PACK, b=2),
             in_=w2_w[:].rearrange("p (m t b) -> p t m b", t=PACK, b=2),
         )
-        tab_w.append(held("tab_w1", [P, T], I32, after="w2_w"))
-        load_words(tab_w[1], tab_words[1])
         v2_scales = held("v2_scales", [P, L], U8)
         nc.vector.tensor_copy(out=v2_scales[:], in_=tab2_plane[:].indirect(offs2_t[:]))
-        wgs_t = held("wgs_t", [P, PACK, L], F32, after="tab2_plane")
+        wgs_rows = wgs.rearrange("(p t) j -> p t j", t=PACK)
+        wgs_first = held("wgs_first", [P, L], F32)
+        wgs_rest = held("wgs_rest", [P, PACK - 1, L], F32)
+        tab_w.append(held("tab_w1", [P, T], I32, after="tab2_plane"))
+        if not EARLY:
+            load_words(tab_w[1], tab_words[1])
         for q in range(4):
-            nc.sync.dma_start(out=wgs_t[32 * q : 32 * q + 32, :, :], in_=wgs.rearrange("(p t) j -> p t j", t=PACK))
+            nc.sync.dma_start(out=wgs_first[32 * q : 32 * q + 32, :], in_=wgs_rows[:, 0, :])
         nc.sync.dma_start(out=pos_t[:], in_=pos1)
+        if EARLY:
+            load_words(tab_w[1], tab_words[1])
+        for q in range(4):
+            nc.sync.dma_start(out=wgs_rest[32 * q : 32 * q + 32, :, :], in_=wgs_rows[:, 1:PACK, :])
         kz_t = held("kz_t", [P, PACK], F32)
         ks_t = held("ks_t", [P, PACK], F32)
         nc.sync.dma_start(out=ks_t[:], in_=ks.rearrange("(p t) -> p t", t=PACK))
@@ -160,8 +183,8 @@ def tile_list_ballast_survival_scorer_kernel(
             )
             b0.append(acc)
         wz_raw = []
-        for u, freed in enumerate(("tab2_w", "w2_plane")):
-            raw = held("wz_raw%d" % u, [P, PACK, N // 2], F32, after=freed)
+        for u in range(2):
+            raw = held("wz_raw%d" % u, [P, PACK, N // 2], F32)
             nc.sync.dma_start(out=raw[:], in_=wz[:, 384 * u : 384 * (u + 1)].rearrange("(p j) c -> p j c", j=PACK))
             wz_raw.append(raw)
         base_rows = base.rearrange("(p t) j -> p t j", t=PACK)
@@ -176,9 +199,8 @@ def tile_list_ballast_survival_scorer_kernel(
         load_base("v2_words")
         ws_w = held("ws_w", [P, N], I32, after="w2_dealt_plane")
         load_words(ws_w, ws_words[0])
-        ws_plane = held("ws_plane", [P, N], U8, after="v2_scales")
         zero_bytes(ws_plane)
-        load_scale_rows(nc.sync, ws_plane, ws_scales)
+        load_scale_rows((nc.sync, nc.sync), ws_plane, ws_scales)
         for t in range(PACK):
             cosine = sine_of(*turns_and_whole(b0[t], 0.25, t, t < KB_V))
             nc.vector.tensor_tensor(out=b[t][:], in0=b0[t][:], in1=cosine[:], op=ALU.max)
@@ -263,7 +285,7 @@ def tile_list_ballast_survival_scorer_kernel(
 
         def scatter(t):
             nc.vector.tensor_tensor(
-                out=placed[t][:].indirect(pos_t[:]), in0=b[t][:], in1=wgs_t[:, t, :], op=ALU.mult
+                out=placed[t][:].indirect(pos_t[:]), in0=b[t][:], in1=wgs_rest[:, t - 1, :] if t else wgs_first[:], op=ALU.mult
             )
 
         def z_part(t, lo, width, top):
@@ -286,9 +308,12 @@ def tile_list_ballast_survival_scorer_kernel(
                 x_part(h, t)
             x_finish(h)
         for t in range(PACK):
-            nc.vector.memset(placed[t][:], 0.0)
+            if t >= PACK - LATE:
+                placed.append(held("placed%d" % t, [P, S], F32, after=("tab2_w", "w2_plane")[t - 2]))
+            zero_bytes(placed[t])
             scatter(t)
-        results = held("results", [P, 12, 2, CHUNK], F32, after="x_rows1")
+        results = held("results", [P, 12 * HALF], F32)
+        used = [0]
 
         out_rows = out.rearrange("(g p) j -> p g j", p=P)
         for c in range(S // CHUNK):
@@ -303,27 +328,33 @@ def tile_list_ballast_survival_scorer_kernel(
                 for t in range(PACK - 1):
                     z_part(t, lo, CHUNK, ring.tile([P, HALF], F32, name="top", bufs=2))
             z_part(PACK - 1, lo, CHUNK, ring.tile([P, HALF], F32, name="top", bufs=2))
-            grouped = held("z_grouped", [P, CHUNK * PACK], BF16, after="x_grouped%d" % h)
-            interleave(nc.scalar.copy if c in ZIL_S else nc.vector.tensor_copy, grouped[:], z_rows[h][:, :, at : at + CHUNK])
-            z_codes = ring.tile([P, CHUNK], U32, name="z_codes", bufs=2, align_bytes=64)
-            z_plane = ring.tile([P, CHUNK], U8, name="z_plane", bufs=2, align_bytes=64)
-            nc.vector.quantize_mx(out=z_codes[:].bitcast(FP8X4), scales=z_plane[:], in_=grouped[:])
-            for g in range(3):
-                acc = bank(Y_BANKS[c][g], "y_%d_%d" % (c, g), [P, 2, CHUNK])
-                for u in range(2):
-                    cols = slice(P * (2 * g + u), P * (2 * g + u + 1))
-                    nc.tensor.matmul_mx(
-                        out=acc[:, u, :], lhsT=ws_w[:, cols].bitcast(FP8X4), lhsT_scale=ws_plane[:, cols],
-                        rhs=x_codes[h][:, at : at + CHUNK].bitcast(FP8X4), rhs_scale=x_plane[h][:, at : at + CHUNK],
-                        start=(u == 0), stop=False,
-                    )
-                for u in range(2):
-                    cols = slice(P * (2 * g + u), P * (2 * g + u + 1))
-                    nc.tensor.matmul_mx(
-                        out=acc[:, u, :], lhsT=wz_codes[:, cols].bitcast(FP8X4), lhsT_scale=wz_plane[:, cols],
-                        rhs=z_codes[:].bitcast(FP8X4), rhs_scale=z_plane[:],
-                        start=False, stop=(u == 1),
-                    )
-                result = results[:, 3 * c + g]
-                nc.scalar.activation(out=result, in_=acc[:], func=ACT.Silu)
-                nc.sync.dma_start(out=out_rows[:, 2 * g : 2 * g + 2, lo : lo + CHUNK], in_=result)
+            for lo2, width, banks in PIECES[c]:
+                at2 = lo2 % HALF
+                grouped = held("z_grouped", [P, width * PACK], BF16, after="x_grouped%d" % h)
+                interleave(nc.scalar.copy if c in ZIL_S else nc.vector.tensor_copy, grouped[:], z_rows[h][:, :, at2 : at2 + width])
+                z_codes = ring.tile([P, width], U32, name="z_codes", bufs=2, align_bytes=64)
+                z_plane = ring.tile([P, width], U8, name="z_plane", bufs=2, align_bytes=64)
+                nc.vector.quantize_mx(out=z_codes[:].bitcast(FP8X4), scales=z_plane[:], in_=grouped[:])
+                per_bank = HALF // width
+                for g, index in enumerate(banks):
+                    tiles = list(range(per_bank * g, min(per_bank * (g + 1), N // P)))
+                    acc = bank(index, "y", [P, len(tiles), width])
+                    for u, i in enumerate(tiles):
+                        cols = slice(P * i, P * (i + 1))
+                        nc.tensor.matmul_mx(
+                            out=acc[:, u, :], lhsT=ws_w[:, cols].bitcast(FP8X4), lhsT_scale=ws_plane[:, cols],
+                            rhs=x_codes[h][:, at2 : at2 + width].bitcast(FP8X4), rhs_scale=x_plane[h][:, at2 : at2 + width],
+                            start=(u == 0), stop=False,
+                        )
+                    for u, i in enumerate(tiles):
+                        cols = slice(P * i, P * (i + 1))
+                        nc.tensor.matmul_mx(
+                            out=acc[:, u, :], lhsT=wz_codes[:, cols].bitcast(FP8X4), lhsT_scale=wz_plane[:, cols],
+                            rhs=z_codes[:].bitcast(FP8X4), rhs_scale=z_plane[:],
+                            start=False, stop=(u == len(tiles) - 1),
+                        )
+                    size = len(tiles) * width
+                    result = results[:, used[0] : used[0] + size].rearrange("p (u j) -> p u j", j=width)
+                    used[0] = used[0] + size
+                    nc.scalar.activation(out=result, in_=acc[:], func=ACT.Silu)
+                    nc.sync.dma_start(out=out_rows[:, tiles[0] : tiles[-1] + 1, lo2 : lo2 + width], in_=result)

@@ -250,8 +250,8 @@ def tile_list_ballast_survival_scorer_kernel(
 
         def interleave(engine_copy, dst, src):
             engine_copy(
-                out=dst.rearrange("p (c i t) -> p c t i", i=4, t=PACK),
-                in_=src.rearrange("p t (c i) -> p c t i", i=4),
+                out=dst.rearrange("p (n t) -> p n t", t=PACK),
+                in_=src.rearrange("p t n -> p n t"),
             )
 
         load_base("w1_raw0")

@@ -3,7 +3,7 @@ from contextlib import ExitStack
 
 import concourse.mybir as mybir
 
-K, K2, T, T3, S, L, H, N = 1024, 512, 4096, 2048, 1024, 512, 512, 768
+K, K2, T, T2, S, L, H, N = 1024, 512, 4096, 2048, 1024, 512, 512, 768
 FLOPS = 2 * (K * H * S + K2 * H * L + 2 * H * N * S)
 
 F32 = mybir.dt.float32
@@ -19,26 +19,14 @@ ACT = mybir.ActivationFunctionType
 
 P = 128
 PACK = 4
+K_PASS = P * PACK
+QUADRANT = 32
+PER_COLUMN = 16
 HALF = 512
 CHUNK = 256
 TWO_PI = 2.0 * math.pi
 ROUNDER = 1.5 * 2.0**23
-KB_V = 2
-KA_V = 0
-XIL_V = ()
-ZIL_S = ()
-GATES = (0, 3, 5)
-TOPS = ("x_rows0", "b0", "x_rows1", "x_rows1")
-Z1_AFTER = "x_rows0"
-FINE = 1
-LATE = 2
-PIECES = (((0, 256, (4, 5, 6)),), ((256, 256, (7, 4, 5)),), ((512, 256, (6, 7, 4)),), ((768, 256, (0, 1, 2)),))
-GATE = "x_rows1"
-TWOQ = 1
-HEAD = "ows2WaOStb"
-EARLY = 1
-ORDER = "atb"
-Y_BANKS = ((4, 5, 6), (7, 4, 5), (0, 1, 2), (3, 6, 7))
+B_WHOLE_ON_VECTOR = 2
 
 
 def tile_list_ballast_survival_scorer_kernel(
@@ -48,113 +36,112 @@ def tile_list_ballast_survival_scorer_kernel(
     nc = tc.nc
     with ExitStack() as ctx:
         keep = ctx.enter_context(tc.tile_pool(name="keep", bufs=1))
-        ring = ctx.enter_context(tc.tile_pool(name="ring", bufs=3))
+        pair = ctx.enter_context(tc.tile_pool(name="pair", bufs=2))
         psum = ctx.enter_context(tc.psum_pool(name="psum", bufs=1))
 
         def held(name, shape, dtype, after=None):
             return keep.tile(shape, dtype, name=name, tag=after or name, align_bytes=64)
 
-        def bank(index, name, shape):
-            return psum.tile(shape, F32, name=name, tag="bank%d" % index)
+        def bank(index, shape):
+            return psum.tile(shape, F32, name="bank%d" % index)
 
-        def zero_bytes(tile):
+        def zero(tile):
             nc.vector.memset(tile[:].bitcast(I32), 0)
 
-        def load_scale_rows(queues, plane, scales):
-            passes = scales.shape[0]
+        def load_plane(plane, scales, second_queue):
+            for r in (0, 2, 1, 3):
+                queue = nc.sync if r < 2 else second_queue
+                queue.dma_start(out=plane[r:P:QUADRANT, :].bitcast(I32), in_=scales[0, r:16:4, :].bitcast(I32))
+
+        def load_two_pass_plane(plane, scales):
             for q in (0, 2, 1, 3):
-                queue = queues[q // 2]
-                if passes == 1:
-                    src = scales[0, 4 * q : 4 * q + 4, :]
-                else:
-                    src = scales[:, 4 * q : 4 * q + 4, :]
-                queue.dma_start(out=plane[32 * q : 32 * q + 4 * passes, :].bitcast(I32), in_=src.bitcast(I32))
+                queue = nc.sync if q < 2 else nc.scalar
+                queue.dma_start(
+                    out=plane[QUADRANT * q : QUADRANT * q + 8, :].bitcast(I32),
+                    in_=scales[:, 4 * q : 4 * q + 4, :].bitcast(I32),
+                )
 
         def load_words(tile, words):
-            nc.sync.dma_start(out=tile[:], in_=words.rearrange("p n t -> p (n t)").bitcast(I32))
+            nc.sync.dma_start(out=tile[:], in_=words.rearrange("p n i -> p (n i)").bitcast(I32))
 
-        offs_t = keep.tile([P, S // 16], U16, name="offs_t")
-        offs2_t = keep.tile([P, L // 16], U16, name="offs2_t")
-        pos_t = keep.tile([P, L // 16], U16, name="pos_t")
-        tab2_plane = held("tab2_plane", [P, T3], U8)
+        def load_rows(tile, rows):
+            nc.sync.dma_start(out=tile[:], in_=rows.rearrange("(p i) c -> p i c", i=PACK))
+
+        def interleave(copy, grouped, rows):
+            copy(
+                out=grouped.rearrange("p (u c i) -> p u i c", c=4, i=PACK),
+                in_=rows.rearrange("p i (u c) -> p u i c", c=4),
+            )
+
+        def quantize(codes, plane, grouped):
+            nc.vector.quantize_mx(out=codes.bitcast(FP8X4), scales=plane, in_=grouped)
+
+        offs_t = keep.tile([P, S // PER_COLUMN], U16, name="offs_t")
+        offs2_t = keep.tile([P, L // PER_COLUMN], U16, name="offs2_t")
+        pos_t = keep.tile([P, L // PER_COLUMN], U16, name="pos_t")
+        tab2_plane = held("tab2_plane", [P, T2], U8)
         w2_plane = held("w2_plane", [P, H], U8)
         tab_plane = held("tab_plane", [P, T], U8)
-        placed = [held("placed%d" % t, [P, S], F32) for t in range(PACK - LATE)]
-        warm = held("warm", [P, 2], F32)
-
-        zero_bytes(tab2_plane)
-        zero_bytes(w2_plane)
-        zero_bytes(tab_plane)
+        placed = [held("placed%d" % t, [P, S], F32) for t in range(2)]
+        zero(tab2_plane)
+        zero(w2_plane)
+        zero(tab_plane)
         ws_plane = held("ws_plane", [P, N], U8)
 
-        tab2_w = held("tab2_w", [P, T3], I32)
+        tab2_w = held("tab2_w", [P, T2], I32)
         w2_w = held("w2_w", [P, 2 * H], U8)
         tab_w = [held("tab_w0", [P, T], I32)]
-        w1_raw = [held("w1_raw%d" % a, [P, PACK, H], F32) for a in range(2)]
-        def big(which):
-            if which == "t":
-                load_words(tab_w[0], tab_words[0])
-            else:
-                a = 0 if which == "a" else 1
-                nc.sync.dma_start(out=w1_raw[a][:], in_=w1[512 * a : 512 * a + 512, :].rearrange("(p j) c -> p j c", j=PACK))
+        w1_raw = [held("w1_raw%d" % g, [P, PACK, H], F32) for g in range(2)]
+        nc.sync.dma_start(out=offs2_t[:], in_=offs2)
+        nc.sync.dma_start(out=w2_w[:].bitcast(I32), in_=w2_words[0].bitcast(I32))
+        load_plane(tab2_plane, tab2_scales, nc.scalar)
+        load_words(tab2_w, tab2_words[0])
+        load_plane(w2_plane, w2_scales, nc.sync)
+        load_rows(w1_raw[0], w1[0:K_PASS, :])
+        nc.sync.dma_start(out=offs_t[:], in_=offs)
+        load_two_pass_plane(tab_plane, tab_scales)
+        load_words(tab_w[0], tab_words[0])
+        load_rows(w1_raw[1], w1[K_PASS:K, :])
 
-        second = nc.scalar if TWOQ else nc.sync
-        for which in HEAD:
-            if which == "o":
-                nc.sync.dma_start(out=offs2_t[:], in_=offs2)
-            elif which == "O":
-                nc.sync.dma_start(out=offs_t[:], in_=offs)
-            elif which == "s":
-                load_scale_rows((nc.sync, second), tab2_plane, tab2_scales)
-            elif which == "S":
-                load_scale_rows((nc.sync, second), tab_plane, tab_scales)
-            elif which == "2":
-                load_words(tab2_w, tab2_words[0])
-            elif which == "w":
-                nc.sync.dma_start(out=w2_w[:].bitcast(I32), in_=w2_words[0].bitcast(I32))
-            elif which == "W":
-                load_scale_rows((nc.sync, nc.sync), w2_plane, w2_scales)
-            else:
-                big(which)
-        nc.vector.memset(warm[:, 0:1], 0.0)
-        nc.scalar.activation(out=warm[:, 1:2], in_=warm[:, 0:1], func=ACT.Silu)
+        zeros = held("zeros", [P, 2], F32)
+        nc.vector.memset(zeros[:, 0:1], 0.0)
+        nc.scalar.activation(out=zeros[:, 1:2], in_=zeros[:, 0:1], func=ACT.Silu)
 
         w2_dealt = held("w2_dealt", [P, 2 * H], U8)
         nc.vector.tensor_copy(
-            out=w2_dealt[:].rearrange("p (t m b) -> p t m b", t=PACK, b=2),
-            in_=w2_w[:].rearrange("p (m t b) -> p t m b", t=PACK, b=2),
+            out=w2_dealt[:].rearrange("p (t m e) -> p t m e", t=PACK, e=2),
+            in_=w2_w[:].rearrange("p (m t e) -> p t m e", t=PACK, e=2),
         )
-        v2_scales = held("v2_scales", [P, L], U8)
-        nc.vector.tensor_copy(out=v2_scales[:], in_=tab2_plane[:].indirect(offs2_t[:]))
+        v2_plane = held("v2_plane", [P, L], U8)
+        nc.vector.tensor_copy(out=v2_plane[:], in_=tab2_plane[:].indirect(offs2_t[:]))
+
         wgs_rows = wgs.rearrange("(p t) j -> p t j", t=PACK)
-        wgs_first = held("wgs_first", [P, L], F32)
+        wgs_first = held("wgs_first", [P, 1, L], F32)
         wgs_rest = held("wgs_rest", [P, PACK - 1, L], F32)
         tab_w.append(held("tab_w1", [P, T], I32, after="tab2_plane"))
-        if not EARLY:
-            load_words(tab_w[1], tab_words[1])
         for q in range(4):
-            nc.sync.dma_start(out=wgs_first[32 * q : 32 * q + 32, :], in_=wgs_rows[:, 0, :])
+            nc.sync.dma_start(out=wgs_first[QUADRANT * q : QUADRANT * (q + 1), :, :], in_=wgs_rows[:, 0:1, :])
         nc.sync.dma_start(out=pos_t[:], in_=pos1)
-        if EARLY:
-            load_words(tab_w[1], tab_words[1])
+        load_words(tab_w[1], tab_words[1])
         for q in range(4):
-            nc.sync.dma_start(out=wgs_rest[32 * q : 32 * q + 32, :, :], in_=wgs_rows[:, 1:PACK, :])
+            nc.sync.dma_start(out=wgs_rest[QUADRANT * q : QUADRANT * (q + 1), :, :], in_=wgs_rows[:, 1:PACK, :])
         kz_t = held("kz_t", [P, PACK], F32)
         ks_t = held("ks_t", [P, PACK], F32)
         nc.sync.dma_start(out=ks_t[:], in_=ks.rearrange("(p t) -> p t", t=PACK))
         nc.sync.dma_start(out=kz_t[:], in_=kz.rearrange("(p t) -> p t", t=PACK))
-        v2_words = held("v2_words", [P, L], U32)
-        nc.vector.tensor_copy(out=v2_words[:], in_=tab2_w[:].bitcast(U32).indirect(offs2_t[:]))
+
+        v2_codes = held("v2_codes", [P, L], U32)
+        nc.vector.tensor_copy(out=v2_codes[:], in_=tab2_w[:].bitcast(U32).indirect(offs2_t[:]))
         w2_dealt_plane = held("w2_dealt_plane", [P, H], U8)
         nc.vector.tensor_copy(
             out=w2_dealt_plane[:].rearrange("p (t m) -> p t m", t=PACK),
             in_=w2_plane[:].rearrange("p (m t) -> p t m", t=PACK),
         )
 
-        def turns_and_whole(acc, shift, slot, on_vector):
-            turns = keep.tile([P, HALF], F32, name="turns", tag="turns%d" % slot)
+        def count_turns(acc, shift, index, on_vector):
+            turns = keep.tile([P, HALF], F32, name="turns%d" % index)
             nc.scalar.activation(out=turns[:], in_=acc[:], func=ACT.Copy, scale=1.0 / TWO_PI, bias=shift)
-            whole = keep.tile([P, HALF], I32, name="whole", tag="whole%d" % slot)
+            whole = keep.tile([P, HALF], I32, name="whole%d" % index)
             if on_vector:
                 nc.vector.tensor_scalar(out=whole[:], in0=turns[:], scalar1=ROUNDER, scalar2=None, op0=ALU.add)
             else:
@@ -163,198 +150,179 @@ def tile_list_ballast_survival_scorer_kernel(
 
         def sine_of(turns, whole):
             nc.vector.scalar_tensor_tensor(
-                out=turns[:], in0=whole[:], scalar=ROUNDER, in1=turns[:],
-                op0=ALU.subtract, op1=ALU.subtract,
+                out=turns[:], in0=whole[:], scalar=ROUNDER, in1=turns[:], op0=ALU.subtract, op1=ALU.subtract
             )
-            nc.scalar.activation(out=turns[:], in_=turns[:], func=ACT.Sin, scale=-TWO_PI)
+            nc.scalar.activation(out=turns[:], in_=turns[:], func=ACT.Sin, scale=-TWO_PI, bias=zeros[:, 1:2])
             return turns
 
         b = [held("b%d" % t, [P, L], F32) for t in range(PACK)]
         b0 = []
         for t in range(PACK):
-            acc = bank(t, "b0_%d" % t, [P, L])
+            acc = bank(t, [P, L])
             nc.tensor.matmul_mx(
                 out=acc[:],
                 lhsT=w2_dealt[:, 2 * P * t : 2 * P * (t + 1)].bitcast(FP4X4),
                 lhsT_scale=w2_dealt_plane[:, P * t : P * (t + 1)],
-                rhs=v2_words[:].bitcast(FP8X4),
-                rhs_scale=v2_scales[:],
-                start=True, stop=True,
+                rhs=v2_codes[:].bitcast(FP8X4),
+                rhs_scale=v2_plane[:],
+                start=True,
+                stop=True,
             )
             b0.append(acc)
-        wz_raw = []
+
+        wz_raw = [held("wz_raw%d" % u, [P, PACK, N // 2], F32) for u in range(2)]
         for u in range(2):
-            raw = held("wz_raw%d" % u, [P, PACK, N // 2], F32)
-            nc.sync.dma_start(out=raw[:], in_=wz[:, 384 * u : 384 * (u + 1)].rearrange("(p j) c -> p j c", j=PACK))
-            wz_raw.append(raw)
+            load_rows(wz_raw[u], wz[:, N // 2 * u : N // 2 * (u + 1)])
         base_rows = base.rearrange("(p t) j -> p t j", t=PACK)
         base_t = []
 
-        def load_base(freed):
-            rows = held("base", [P, S], F32, after=freed)
+        def load_base(after):
+            rows = held("base", [P, S], F32, after=after)
             nc.sync.dma_start(out=rows[:], in_=base_rows[:, len(base_t), :])
             base_t.append(rows)
 
         load_base("w2_dealt")
-        load_base("v2_words")
+        load_base("v2_codes")
         ws_w = held("ws_w", [P, N], I32, after="w2_dealt_plane")
         load_words(ws_w, ws_words[0])
-        zero_bytes(ws_plane)
-        load_scale_rows((nc.sync, nc.sync), ws_plane, ws_scales)
+        zero(ws_plane)
+        load_plane(ws_plane, ws_scales, nc.sync)
+
         for t in range(PACK):
-            cosine = sine_of(*turns_and_whole(b0[t], 0.25, t, t < KB_V))
+            cosine = sine_of(*count_turns(b0[t], 0.25, t, t < B_WHOLE_ON_VECTOR))
             nc.vector.tensor_tensor(out=b[t][:], in0=b0[t][:], in1=cosine[:], op=ALU.max)
 
-        w1_codes, w1_plane, v_words = [], [], []
-        w1_grouped = held("grouped", [P, 2, H * PACK], BF16)
-        v_scales = held("v_scales", [P, S], U8)
+        list_half = [offs_t[:, HALF // PER_COLUMN * h : HALF // PER_COLUMN * (h + 1)] for h in range(2)]
+        w1_grouped = held("w1_grouped", [P, 2, H * PACK], BF16)
+        v_plane = held("v_plane", [P, S], U8)
         for h in range(2):
-            nc.vector.tensor_copy(
-                out=v_scales[:, HALF * h : HALF * (h + 1)], in_=tab_plane[:].indirect(offs_t[:, 32 * h : 32 * h + 32])
-            )
-        for a in range(2):
-            grouped = w1_grouped[:, a, :]
-            for m0 in (0, 64):
+            nc.vector.tensor_copy(out=v_plane[:, HALF * h : HALF * (h + 1)], in_=tab_plane[:].indirect(list_half[h]))
+        w1_codes, w1_plane, v_codes = [], [], []
+        for g in range(2):
+            for m0 in (0, P // 2):
                 nc.scalar.copy(
-                    out=grouped.rearrange("p (t m j) -> p m t j", t=PACK, j=PACK)[:, m0 : m0 + 64],
-                    in_=w1_raw[a][:].rearrange("p j (m t) -> p m t j", t=PACK)[:, m0 : m0 + 64],
+                    out=w1_grouped[:, g, :].rearrange("p (t m i) -> p m t i", t=PACK, i=PACK)[:, m0 : m0 + P // 2],
+                    in_=w1_raw[g][:].rearrange("p i (m t) -> p m t i", t=PACK)[:, m0 : m0 + P // 2],
                 )
-            codes = held("w1_codes%d" % a, [P, H], U32)
-            plane = held("w1_plane%d" % a, [P, H], U8)
-            nc.vector.quantize_mx(out=codes[:].bitcast(FP8X4), scales=plane[:], in_=grouped)
-            w1_codes.append(codes)
-            w1_plane.append(plane)
-            halves = []
+            w1_codes.append(held("w1_codes%d" % g, [P, H], U32))
+            w1_plane.append(held("w1_plane%d" % g, [P, H], U8))
+            quantize(w1_codes[g][:], w1_plane[g][:], w1_grouped[:, g, :])
+            v_codes.append([held("v_codes%d_%d" % (g, h), [P, HALF], U32) for h in range(2)])
             for h in range(2):
-                words = held("v_words%d_%d" % (a, h), [P, HALF], U32)
-                nc.vector.tensor_copy(
-                    out=words[:], in_=tab_w[a][:].bitcast(U32).indirect(offs_t[:, 32 * h : 32 * h + 32])
-                )
-                halves.append(words)
-            v_words.append(halves)
+                nc.vector.tensor_copy(out=v_codes[g][h][:], in_=tab_w[g][:].bitcast(U32).indirect(list_half[h]))
 
-        a_acc = {}
+        a = {}
         for h in range(2):
             for t in range(PACK):
-                acc = bank(4 * (1 - h) + t, "a_%d_%d" % (h, t), [P, HALF])
-                for a in range(2):
+                acc = bank(PACK * (1 - h) + t, [P, HALF])
+                for g in range(2):
                     nc.tensor.matmul_mx(
                         out=acc[:],
-                        lhsT=w1_codes[a][:, P * t : P * (t + 1)].bitcast(FP8X4),
-                        lhsT_scale=w1_plane[a][:, P * t : P * (t + 1)],
-                        rhs=v_words[a][h][:].bitcast(FP8X4),
-                        rhs_scale=v_scales[4 * a : P, HALF * h : HALF * (h + 1)],
-                        start=(a == 0), stop=(a == 1),
+                        lhsT=w1_codes[g][:, P * t : P * (t + 1)].bitcast(FP8X4),
+                        lhsT_scale=w1_plane[g][:, P * t : P * (t + 1)],
+                        rhs=v_codes[g][h][:].bitcast(FP8X4),
+                        rhs_scale=v_plane[4 * g : P, HALF * h : HALF * (h + 1)],
+                        start=(g == 0),
+                        stop=(g == 1),
                     )
-                a_acc[(h, t)] = acc
-
-        def interleave(engine_copy, dst, src):
-            engine_copy(
-                out=dst.rearrange("p (n t) -> p n t", t=PACK),
-                in_=src.rearrange("p t n -> p n t"),
-            )
+                a[(h, t)] = acc
 
         load_base("w1_raw0")
         load_base("w1_raw1")
         wz_grouped = held("wz_grouped", [P, N * PACK], BF16)
         wz_codes = held("wz_codes", [P, N], U32)
         wz_plane = held("wz_plane", [P, N], U8)
-
-        def prepare_wz():
-            for u in range(2):
-                interleave(nc.scalar.copy, wz_grouped[:, 1536 * u : 1536 * (u + 1)], wz_raw[u][:])
-            for lo, hi in ((0, 512), (512, 768)):
-                nc.vector.quantize_mx(
-                    out=wz_codes[:, lo:hi].bitcast(FP8X4), scales=wz_plane[:, lo:hi],
-                    in_=wz_grouped[:, PACK * lo : PACK * hi],
-                )
-
         x_rows = [held("x_rows%d" % h, [P, PACK, HALF], BF16) for h in range(2)]
         z_rows = [held("z_rows0", [P, PACK, HALF], BF16)]
         x_codes = [held("x_codes%d" % h, [P, HALF], U32) for h in range(2)]
         x_plane = [held("x_plane%d" % h, [P, HALF], U8) for h in range(2)]
 
-        def x_part(h, t):
-            sine = sine_of(*reduced[(h, t)])
-            nc.scalar.activation(out=x_rows[h][:, t, :], in_=sine[:], func=ACT.Copy, scale=ks_t[:, t : t + 1])
+        counted = {}
+        for h in range(2):
+            for t in range(PACK):
+                counted[(h, t)] = count_turns(a[(h, t)], 0.0, PACK * h + t, False)
+        for u in range(2):
+            interleave(nc.scalar.copy, wz_grouped[:, N // 2 * PACK * u : N // 2 * PACK * (u + 1)], wz_raw[u][:])
+        for lo, hi in ((0, 512), (512, N)):
+            quantize(wz_codes[:, lo:hi], wz_plane[:, lo:hi], wz_grouped[:, PACK * lo : PACK * hi])
+        for h in range(2):
+            for t in range(PACK):
+                sine = sine_of(*counted[(h, t)])
+                nc.scalar.activation(out=x_rows[h][:, t, :], in_=sine[:], func=ACT.Copy, scale=ks_t[:, t : t + 1])
+            x_grouped = held("x_grouped%d" % h, [P, HALF * PACK], BF16)
+            interleave(nc.scalar.copy, x_grouped[:], x_rows[h][:])
+            quantize(x_codes[h][:], x_plane[h][:], x_grouped[:])
 
-        def x_finish(h):
-            grouped = held("x_grouped%d" % h, [P, HALF * PACK], BF16)
-            interleave(nc.vector.tensor_copy if h in XIL_V else nc.scalar.copy, grouped[:], x_rows[h][:])
-            nc.vector.quantize_mx(out=x_codes[h][:].bitcast(FP8X4), scales=x_plane[h][:], in_=grouped[:])
-
-        def scatter(t):
+        placed.append(held("placed2", [P, S], F32, after="tab2_w"))
+        placed.append(held("placed3", [P, S], F32, after="w2_plane"))
+        for t in range(PACK):
+            zero(placed[t])
             nc.vector.tensor_tensor(
-                out=placed[t][:].indirect(pos_t[:]), in0=b[t][:], in1=wgs_rest[:, t - 1, :] if t else wgs_first[:], op=ALU.mult
+                out=placed[t][:].indirect(pos_t[:]),
+                in0=b[t][:],
+                in1=wgs_rest[:, t - 1, :] if t else wgs_first[:, 0, :],
+                op=ALU.mult,
             )
 
-        def z_part(t, lo, width, top):
+        def z_part(t, lo, width):
             h, at = divmod(lo, HALF)
+            top = pair.tile([P, HALF], F32, name="top")
             nc.vector.tensor_tensor(
-                out=top[:, 0:width], in0=a_acc[(h, t)][:, at : at + width], in1=placed[t][:, lo : lo + width], op=ALU.max
+                out=top[:, 0:width], in0=a[(h, t)][:, at : at + width], in1=placed[t][:, lo : lo + width], op=ALU.max
             )
             nc.vector.scalar_tensor_tensor(
-                out=z_rows[h][:, t, at : at + width], in0=top[:, 0:width], scalar=kz_t[:, t : t + 1],
-                in1=base_t[t][:, lo : lo + width], op0=ALU.mult, op1=ALU.add,
+                out=z_rows[h][:, t, at : at + width],
+                in0=top[:, 0:width],
+                scalar=kz_t[:, t : t + 1],
+                in1=base_t[t][:, lo : lo + width],
+                op0=ALU.mult,
+                op1=ALU.add,
             )
 
-        reduced = {}
-        for h in range(2):
-            for t in range(PACK):
-                reduced[(h, t)] = turns_and_whole(a_acc[(h, t)], 0.0, PACK * h + t, PACK * h + t < KA_V)
-        prepare_wz()
-        for h in range(2):
-            for t in range(PACK):
-                x_part(h, t)
-            x_finish(h)
-        for t in range(PACK):
-            if t >= PACK - LATE:
-                placed.append(held("placed%d" % t, [P, S], F32, after=("tab2_w", "w2_plane")[t - 2]))
-            zero_bytes(placed[t])
-            scatter(t)
-        results = held("results", [P, 12 * HALF], F32)
-        used = [0]
-
-        out_rows = out.rearrange("(g p) j -> p g j", p=P)
+        results = held("results", [P, S // CHUNK, N // P, CHUNK], F32)
+        out_rows = out.rearrange("(u p) j -> p u j", p=P)
+        banks_per_chunk = N // P // 2
         for c in range(S // CHUNK):
             lo = CHUNK * c
             h, at = divmod(lo, HALF)
             if c == 2:
-                z_rows.append(held("z_rows1", [P, PACK, HALF], BF16, after=Z1_AFTER))
-            if c == 0 or (c == 2 and not FINE):
-                for t in range(PACK - 1):
-                    z_part(t, lo, HALF, ring.tile([P, HALF], F32, name="top", bufs=2))
-            if h == 1 and FINE:
-                for t in range(PACK - 1):
-                    z_part(t, lo, CHUNK, ring.tile([P, HALF], F32, name="top", bufs=2))
-            z_part(PACK - 1, lo, CHUNK, ring.tile([P, HALF], F32, name="top", bufs=2))
-            for lo2, width, banks in PIECES[c]:
-                at2 = lo2 % HALF
-                grouped = held("z_grouped", [P, width * PACK], BF16, after="x_grouped%d" % h)
-                interleave(nc.scalar.copy if c in ZIL_S else nc.vector.tensor_copy, grouped[:], z_rows[h][:, :, at2 : at2 + width])
-                z_codes = ring.tile([P, width], U32, name="z_codes", bufs=2, align_bytes=64)
-                z_plane = ring.tile([P, width], U8, name="z_plane", bufs=2, align_bytes=64)
-                nc.vector.quantize_mx(out=z_codes[:].bitcast(FP8X4), scales=z_plane[:], in_=grouped[:])
-                per_bank = HALF // width
-                for g, index in enumerate(banks):
-                    tiles = list(range(per_bank * g, min(per_bank * (g + 1), N // P)))
-                    acc = bank(index, "y", [P, len(tiles), width])
-                    for u, i in enumerate(tiles):
-                        cols = slice(P * i, P * (i + 1))
-                        nc.tensor.matmul_mx(
-                            out=acc[:, u, :], lhsT=ws_w[:, cols].bitcast(FP8X4), lhsT_scale=ws_plane[:, cols],
-                            rhs=x_codes[h][:, at2 : at2 + width].bitcast(FP8X4), rhs_scale=x_plane[h][:, at2 : at2 + width],
-                            start=(u == 0), stop=False,
-                        )
-                    for u, i in enumerate(tiles):
-                        cols = slice(P * i, P * (i + 1))
-                        nc.tensor.matmul_mx(
-                            out=acc[:, u, :], lhsT=wz_codes[:, cols].bitcast(FP8X4), lhsT_scale=wz_plane[:, cols],
-                            rhs=z_codes[:].bitcast(FP8X4), rhs_scale=z_plane[:],
-                            start=False, stop=(u == len(tiles) - 1),
-                        )
-                    size = len(tiles) * width
-                    result = results[:, used[0] : used[0] + size].rearrange("p (u j) -> p u j", j=width)
-                    used[0] = used[0] + size
-                    nc.scalar.activation(out=result, in_=acc[:], func=ACT.Silu)
-                    nc.sync.dma_start(out=out_rows[:, tiles[0] : tiles[-1] + 1, lo2 : lo2 + width], in_=result)
+                z_rows.append(held("z_rows1", [P, PACK, HALF], BF16, after="x_rows0"))
+            for t in range(PACK - 1):
+                if c == 0:
+                    z_part(t, lo, HALF)
+                if h == 1:
+                    z_part(t, lo, CHUNK)
+            z_part(PACK - 1, lo, CHUNK)
+            z_grouped = held("z_grouped", [P, CHUNK * PACK], BF16, after="x_grouped%d" % h)
+            interleave(nc.vector.tensor_copy, z_grouped[:], z_rows[h][:, :, at : at + CHUNK])
+            z_codes = pair.tile([P, CHUNK], U32, name="z_codes", align_bytes=64)
+            z_plane = pair.tile([P, CHUNK], U8, name="z_plane", align_bytes=64)
+            quantize(z_codes[:], z_plane[:], z_grouped[:])
+            for s in range(banks_per_chunk):
+                last = c == S // CHUNK - 1
+                acc = bank(s if last else PACK + (banks_per_chunk * c + s) % PACK, [P, 2, CHUNK])
+                for u in range(2):
+                    cols = slice(P * (2 * s + u), P * (2 * s + u + 1))
+                    nc.tensor.matmul_mx(
+                        out=acc[:, u, :],
+                        lhsT=ws_w[:, cols].bitcast(FP8X4),
+                        lhsT_scale=ws_plane[:, cols],
+                        rhs=x_codes[h][:, at : at + CHUNK].bitcast(FP8X4),
+                        rhs_scale=x_plane[h][:, at : at + CHUNK],
+                        start=(u == 0),
+                        stop=False,
+                    )
+                for u in range(2):
+                    cols = slice(P * (2 * s + u), P * (2 * s + u + 1))
+                    nc.tensor.matmul_mx(
+                        out=acc[:, u, :],
+                        lhsT=wz_codes[:, cols].bitcast(FP8X4),
+                        lhsT_scale=wz_plane[:, cols],
+                        rhs=z_codes[:].bitcast(FP8X4),
+                        rhs_scale=z_plane[:],
+                        start=False,
+                        stop=(u == 1),
+                    )
+                result = results[:, c, 2 * s : 2 * s + 2, :]
+                nc.scalar.activation(out=result, in_=acc[:], func=ACT.Silu)
+                nc.sync.dma_start(out=out_rows[:, 2 * s : 2 * s + 2, lo : lo + CHUNK], in_=result)

import math
from contextlib import ExitStack

import concourse.mybir as mybir

K, K2, T, T2, S, L, H, N = 1024, 512, 4096, 2048, 1024, 512, 512, 768
FLOPS = 2 * (K * H * S + K2 * H * L + 2 * H * N * S)

F32 = mybir.dt.float32
BF16 = mybir.dt.bfloat16
I32 = mybir.dt.int32
U32 = mybir.dt.uint32
U16 = mybir.dt.uint16
U8 = mybir.dt.uint8
FP8X4 = mybir.dt.float8_e4m3fn_x4
FP4X4 = mybir.dt.float4_e2m1fn_x4
ALU = mybir.AluOpType
ACT = mybir.ActivationFunctionType

P = 128
PACK = 4
K_PASS = P * PACK
QUADRANT = 32
PER_COLUMN = 16
HALF = 512
CHUNK = 256
TWO_PI = 2.0 * math.pi
ROUNDER = 1.5 * 2.0**23
B_WHOLE_ON_VECTOR = 2


def tile_list_ballast_survival_scorer_kernel(
    tc, tab_words, tab_scales, tab2_words, tab2_scales, offs, offs2, pos1, w1,
    w2_words, w2_scales, wgs, kz, base, ks, wz, ws_words, ws_scales, out,
):
    nc = tc.nc
    with ExitStack() as ctx:
        keep = ctx.enter_context(tc.tile_pool(name="keep", bufs=1))
        pair = ctx.enter_context(tc.tile_pool(name="pair", bufs=2))
        psum = ctx.enter_context(tc.psum_pool(name="psum", bufs=1))

        def held(name, shape, dtype, after=None):
            return keep.tile(shape, dtype, name=name, tag=after or name, align_bytes=64)

        def bank(index, shape):
            return psum.tile(shape, F32, name="bank%d" % index)

        def zero(tile):
            nc.vector.memset(tile[:].bitcast(I32), 0)

        def load_plane(plane, scales, second_queue):
            for r in (0, 2, 1, 3):
                queue = nc.sync if r < 2 else second_queue
                queue.dma_start(out=plane[r:P:QUADRANT, :].bitcast(I32), in_=scales[0, r:16:4, :].bitcast(I32))

        def load_two_pass_plane(plane, scales):
            for q in (0, 2, 1, 3):
                queue = nc.sync if q < 2 else nc.scalar
                queue.dma_start(
                    out=plane[QUADRANT * q : QUADRANT * q + 8, :].bitcast(I32),
                    in_=scales[:, 4 * q : 4 * q + 4, :].bitcast(I32),
                )

        def load_words(tile, words):
            nc.sync.dma_start(out=tile[:], in_=words.rearrange("p n i -> p (n i)").bitcast(I32))

        def load_rows(tile, rows):
            nc.sync.dma_start(out=tile[:], in_=rows.rearrange("(p i) c -> p i c", i=PACK))

        def interleave(copy, grouped, rows):
            copy(
                out=grouped.rearrange("p (u c i) -> p u i c", c=4, i=PACK),
                in_=rows.rearrange("p i (u c) -> p u i c", c=4),
            )

        def quantize(codes, plane, grouped):
            nc.vector.quantize_mx(out=codes.bitcast(FP8X4), scales=plane, in_=grouped)

        offs_t = keep.tile([P, S // PER_COLUMN], U16, name="offs_t")
        offs2_t = keep.tile([P, L // PER_COLUMN], U16, name="offs2_t")
        pos_t = keep.tile([P, L // PER_COLUMN], U16, name="pos_t")
        tab2_plane = held("tab2_plane", [P, T2], U8)
        w2_plane = held("w2_plane", [P, H], U8)
        tab_plane = held("tab_plane", [P, T], U8)
        placed = [held("placed%d" % t, [P, S], F32) for t in range(2)]
        zero(tab2_plane)
        zero(w2_plane)
        zero(tab_plane)
        ws_plane = held("ws_plane", [P, N], U8)

        tab2_w = held("tab2_w", [P, T2], I32)
        w2_w = held("w2_w", [P, 2 * H], U8)
        tab_w = [held("tab_w0", [P, T], I32)]
        w1_raw = [held("w1_raw%d" % g, [P, PACK, H], F32) for g in range(2)]
        nc.sync.dma_start(out=offs2_t[:], in_=offs2)
        nc.sync.dma_start(out=w2_w[:].bitcast(I32), in_=w2_words[0].bitcast(I32))
        load_plane(tab2_plane, tab2_scales, nc.scalar)
        load_words(tab2_w, tab2_words[0])
        load_plane(w2_plane, w2_scales, nc.sync)
        load_rows(w1_raw[0], w1[0:K_PASS, :])
        nc.sync.dma_start(out=offs_t[:], in_=offs)
        load_two_pass_plane(tab_plane, tab_scales)
        load_words(tab_w[0], tab_words[0])
        load_rows(w1_raw[1], w1[K_PASS:K, :])

        zeros = held("zeros", [P, 2], F32)
        nc.vector.memset(zeros[:, 0:1], 0.0)
        nc.scalar.activation(out=zeros[:, 1:2], in_=zeros[:, 0:1], func=ACT.Silu)

        w2_dealt = held("w2_dealt", [P, 2 * H], U8)
        nc.vector.tensor_copy(
            out=w2_dealt[:].rearrange("p (t m e) -> p t m e", t=PACK, e=2),
            in_=w2_w[:].rearrange("p (m t e) -> p t m e", t=PACK, e=2),
        )
        v2_plane = held("v2_plane", [P, L], U8)
        nc.vector.tensor_copy(out=v2_plane[:], in_=tab2_plane[:].indirect(offs2_t[:]))

        wgs_rows = wgs.rearrange("(p t) j -> p t j", t=PACK)
        wgs_first = held("wgs_first", [P, 1, L], F32)
        wgs_rest = held("wgs_rest", [P, PACK - 1, L], F32)
        tab_w.append(held("tab_w1", [P, T], I32, after="tab2_plane"))
        for q in range(4):
            nc.sync.dma_start(out=wgs_first[QUADRANT * q : QUADRANT * (q + 1), :, :], in_=wgs_rows[:, 0:1, :])
        nc.sync.dma_start(out=pos_t[:], in_=pos1)
        load_words(tab_w[1], tab_words[1])
        for q in range(4):
            nc.sync.dma_start(out=wgs_rest[QUADRANT * q : QUADRANT * (q + 1), :, :], in_=wgs_rows[:, 1:PACK, :])
        kz_t = held("kz_t", [P, PACK], F32)
        ks_t = held("ks_t", [P, PACK], F32)
        nc.sync.dma_start(out=ks_t[:], in_=ks.rearrange("(p t) -> p t", t=PACK))
        nc.sync.dma_start(out=kz_t[:], in_=kz.rearrange("(p t) -> p t", t=PACK))

        v2_codes = held("v2_codes", [P, L], U32)
        nc.vector.tensor_copy(out=v2_codes[:], in_=tab2_w[:].bitcast(U32).indirect(offs2_t[:]))
        w2_dealt_plane = held("w2_dealt_plane", [P, H], U8)
        nc.vector.tensor_copy(
            out=w2_dealt_plane[:].rearrange("p (t m) -> p t m", t=PACK),
            in_=w2_plane[:].rearrange("p (m t) -> p t m", t=PACK),
        )

        def count_turns(acc, shift, index, on_vector):
            turns = keep.tile([P, HALF], F32, name="turns%d" % index)
            nc.scalar.activation(out=turns[:], in_=acc[:], func=ACT.Copy, scale=1.0 / TWO_PI, bias=shift)
            whole = keep.tile([P, HALF], I32, name="whole%d" % index)
            if on_vector:
                nc.vector.tensor_scalar(out=whole[:], in0=turns[:], scalar1=ROUNDER, scalar2=None, op0=ALU.add)
            else:
                nc.scalar.activation(out=whole[:].bitcast(U32), in_=turns[:], func=ACT.Copy, bias=ROUNDER)
            return turns, whole

        def sine_of(turns, whole):
            nc.vector.scalar_tensor_tensor(
                out=turns[:], in0=whole[:], scalar=ROUNDER, in1=turns[:], op0=ALU.subtract, op1=ALU.subtract
            )
            nc.scalar.activation(out=turns[:], in_=turns[:], func=ACT.Sin, scale=-TWO_PI, bias=zeros[:, 1:2])
            return turns

        b = [held("b%d" % t, [P, L], F32) for t in range(PACK)]
        b0 = []
        for t in range(PACK):
            acc = bank(t, [P, L])
            nc.tensor.matmul_mx(
                out=acc[:],
                lhsT=w2_dealt[:, 2 * P * t : 2 * P * (t + 1)].bitcast(FP4X4),
                lhsT_scale=w2_dealt_plane[:, P * t : P * (t + 1)],
                rhs=v2_codes[:].bitcast(FP8X4),
                rhs_scale=v2_plane[:],
                start=True,
                stop=True,
            )
            b0.append(acc)

        wz_raw = [held("wz_raw%d" % u, [P, PACK, N // 2], F32) for u in range(2)]
        for u in range(2):
            load_rows(wz_raw[u], wz[:, N // 2 * u : N // 2 * (u + 1)])
        base_rows = base.rearrange("(p t) j -> p t j", t=PACK)
        base_t = []

        def load_base(after):
            rows = held("base", [P, S], F32, after=after)
            nc.sync.dma_start(out=rows[:], in_=base_rows[:, len(base_t), :])
            base_t.append(rows)

        load_base("w2_dealt")
        load_base("v2_codes")
        ws_w = held("ws_w", [P, N], I32, after="w2_dealt_plane")
        load_words(ws_w, ws_words[0])
        zero(ws_plane)
        load_plane(ws_plane, ws_scales, nc.sync)

        for t in range(PACK):
            cosine = sine_of(*count_turns(b0[t], 0.25, t, t < B_WHOLE_ON_VECTOR))
            nc.vector.tensor_tensor(out=b[t][:], in0=b0[t][:], in1=cosine[:], op=ALU.max)

        list_half = [offs_t[:, HALF // PER_COLUMN * h : HALF // PER_COLUMN * (h + 1)] for h in range(2)]
        w1_grouped = held("w1_grouped", [P, 2, H * PACK], BF16)
        v_plane = held("v_plane", [P, S], U8)
        for h in range(2):
            nc.vector.tensor_copy(out=v_plane[:, HALF * h : HALF * (h + 1)], in_=tab_plane[:].indirect(list_half[h]))
        w1_codes, w1_plane, v_codes = [], [], []
        for g in range(2):
            for m0 in (0, P // 2):
                nc.scalar.copy(
                    out=w1_grouped[:, g, :].rearrange("p (t m i) -> p m t i", t=PACK, i=PACK)[:, m0 : m0 + P // 2],
                    in_=w1_raw[g][:].rearrange("p i (m t) -> p m t i", t=PACK)[:, m0 : m0 + P // 2],
                )
            w1_codes.append(held("w1_codes%d" % g, [P, H], U32))
            w1_plane.append(held("w1_plane%d" % g, [P, H], U8))
            quantize(w1_codes[g][:], w1_plane[g][:], w1_grouped[:, g, :])
            v_codes.append([held("v_codes%d_%d" % (g, h), [P, HALF], U32) for h in range(2)])
            for h in range(2):
                nc.vector.tensor_copy(out=v_codes[g][h][:], in_=tab_w[g][:].bitcast(U32).indirect(list_half[h]))

        a = {}
        for h in range(2):
            for t in range(PACK):
                acc = bank(PACK * (1 - h) + t, [P, HALF])
                for g in range(2):
                    nc.tensor.matmul_mx(
                        out=acc[:],
                        lhsT=w1_codes[g][:, P * t : P * (t + 1)].bitcast(FP8X4),
                        lhsT_scale=w1_plane[g][:, P * t : P * (t + 1)],
                        rhs=v_codes[g][h][:].bitcast(FP8X4),
                        rhs_scale=v_plane[4 * g : P, HALF * h : HALF * (h + 1)],
                        start=(g == 0),
                        stop=(g == 1),
                    )
                a[(h, t)] = acc

        load_base("w1_raw0")
        load_base("w1_raw1")
        wz_grouped = held("wz_grouped", [P, N * PACK], BF16)
        wz_codes = held("wz_codes", [P, N], U32)
        wz_plane = held("wz_plane", [P, N], U8)
        x_rows = [held("x_rows%d" % h, [P, PACK, HALF], BF16) for h in range(2)]
        z_rows = [held("z_rows0", [P, PACK, HALF], BF16)]
        x_codes = [held("x_codes%d" % h, [P, HALF], U32) for h in range(2)]
        x_plane = [held("x_plane%d" % h, [P, HALF], U8) for h in range(2)]

        counted = {}
        for h in range(2):
            for t in range(PACK):
                counted[(h, t)] = count_turns(a[(h, t)], 0.0, PACK * h + t, False)
        for u in range(2):
            interleave(nc.scalar.copy, wz_grouped[:, N // 2 * PACK * u : N // 2 * PACK * (u + 1)], wz_raw[u][:])
        for lo, hi in ((0, 512), (512, N)):
            quantize(wz_codes[:, lo:hi], wz_plane[:, lo:hi], wz_grouped[:, PACK * lo : PACK * hi])
        for h in range(2):
            for t in range(PACK):
                sine = sine_of(*counted[(h, t)])
                nc.scalar.activation(out=x_rows[h][:, t, :], in_=sine[:], func=ACT.Copy, scale=ks_t[:, t : t + 1])
            x_grouped = held("x_grouped%d" % h, [P, HALF * PACK], BF16)
            interleave(nc.scalar.copy, x_grouped[:], x_rows[h][:])
            quantize(x_codes[h][:], x_plane[h][:], x_grouped[:])

        placed.append(held("placed2", [P, S], F32, after="tab2_w"))
        placed.append(held("placed3", [P, S], F32, after="w2_plane"))
        for t in range(PACK):
            zero(placed[t])
            nc.vector.tensor_tensor(
                out=placed[t][:].indirect(pos_t[:]),
                in0=b[t][:],
                in1=wgs_rest[:, t - 1, :] if t else wgs_first[:, 0, :],
                op=ALU.mult,
            )

        def z_part(t, lo, width):
            h, at = divmod(lo, HALF)
            top = pair.tile([P, HALF], F32, name="top")
            nc.vector.tensor_tensor(
                out=top[:, 0:width], in0=a[(h, t)][:, at : at + width], in1=placed[t][:, lo : lo + width], op=ALU.max
            )
            nc.vector.scalar_tensor_tensor(
                out=z_rows[h][:, t, at : at + width],
                in0=top[:, 0:width],
                scalar=kz_t[:, t : t + 1],
                in1=base_t[t][:, lo : lo + width],
                op0=ALU.mult,
                op1=ALU.add,
            )

        results = held("results", [P, S // CHUNK, N // P, CHUNK], F32)
        out_rows = out.rearrange("(u p) j -> p u j", p=P)
        banks_per_chunk = N // P // 2
        for c in range(S // CHUNK):
            lo = CHUNK * c
            h, at = divmod(lo, HALF)
            if c == 2:
                z_rows.append(held("z_rows1", [P, PACK, HALF], BF16, after="x_rows0"))
            for t in range(PACK - 1):
                if c == 0:
                    z_part(t, lo, HALF)
                if h == 1:
                    z_part(t, lo, CHUNK)
            z_part(PACK - 1, lo, CHUNK)
            z_grouped = held("z_grouped", [P, CHUNK * PACK], BF16, after="x_grouped%d" % h)
            interleave(nc.vector.tensor_copy, z_grouped[:], z_rows[h][:, :, at : at + CHUNK])
            z_codes = pair.tile([P, CHUNK], U32, name="z_codes", align_bytes=64)
            z_plane = pair.tile([P, CHUNK], U8, name="z_plane", align_bytes=64)
            quantize(z_codes[:], z_plane[:], z_grouped[:])
            for s in range(banks_per_chunk):
                last = c == S // CHUNK - 1
                acc = bank(s if last else PACK + (banks_per_chunk * c + s) % PACK, [P, 2, CHUNK])
                for u in range(2):
                    cols = slice(P * (2 * s + u), P * (2 * s + u + 1))
                    nc.tensor.matmul_mx(
                        out=acc[:, u, :],
                        lhsT=ws_w[:, cols].bitcast(FP8X4),
                        lhsT_scale=ws_plane[:, cols],
                        rhs=x_codes[h][:, at : at + CHUNK].bitcast(FP8X4),
                        rhs_scale=x_plane[h][:, at : at + CHUNK],
                        start=(u == 0),
                        stop=False,
                    )
                for u in range(2):
                    cols = slice(P * (2 * s + u), P * (2 * s + u + 1))
                    nc.tensor.matmul_mx(
                        out=acc[:, u, :],
                        lhsT=wz_codes[:, cols].bitcast(FP8X4),
                        lhsT_scale=wz_plane[:, cols],
                        rhs=z_codes[:].bitcast(FP8X4),
                        rhs_scale=z_plane[:],
                        start=False,
                        stop=(u == 1),
                    )
                result = results[:, c, 2 * s : 2 * s + 2, :]
                nc.scalar.activation(out=result, in_=acc[:], func=ACT.Silu)
                nc.sync.dma_start(out=out_rows[:, 2 * s : 2 * s + 2, lo : lo + CHUNK], in_=result)
